import numpy as np
import ml_dtypes


def mxq(x, axis, fmt="e4m3"):
    dtype, down = {"e4m3": (ml_dtypes.float8_e4m3fn, 7), "e5m2": (ml_dtypes.float8_e5m2, 14)}[fmt]
    v = np.moveaxis(np.asarray(x, np.float32).astype(ml_dtypes.bfloat16).astype(np.float64), axis, -1)
    blocks = v.reshape(v.shape[:-1] + (-1, 32))
    amax = np.abs(blocks).max(-1, keepdims=True)
    byte = np.maximum(np.where(amax > 0, np.frexp(amax)[1] - 1 + 127, 0) - down, 1)
    scale = np.exp2(byte - 127.0)
    codes = (blocks / scale).astype(np.float32).astype(dtype).astype(np.float64)
    return np.moveaxis((codes * scale).reshape(v.shape), -1, axis)


WIDE = False


def mx_kscale(k):
    if not WIDE:
        return np.ones(k)
    levels = np.array([10, -10, 5, -5, 0])
    if k % 512:
        return np.exp2(np.random.permutation(np.resize(levels, k // 32))).repeat(32)
    a = np.empty((k // 512, 16))
    for p in range(k // 512):
        a[p, :8] = np.random.permutation(np.resize(levels, 8))
        for g in range(8):
            far = levels[np.abs(levels - a[p, g]) >= 10]
            a[p, g + 8] = far[np.random.randint(len(far))]
    return np.exp2(a.ravel()).repeat(32)


BF16 = ml_dtypes.bfloat16


def bf(x):
    return np.asarray(x, np.float32).astype(BF16)


def f64(x):
    return np.asarray(x).astype(np.float64)

E4M3FN = np.array([(-1.0 if i & 128 else 1.0) * ((1.0 + (i & 7) / 8.0) * 2.0 ** (((i >> 3) & 15) - 7) if i & 120 else (i & 7) * 2.0 ** -9) for i in range(256)])


def e4m3fn_bytes(y):
    return np.clip(np.asarray(y, np.float64), -448.0, 448.0).astype(np.float32).astype(ml_dtypes.float8_e4m3fn).view(np.uint8)


def e4m3fn_values(b):
    return E4M3FN[b]


N, T, K, B = 2048, 2048, 512, 128


def setup_inputs():
    s = mx_kscale(K)
    C = np.random.standard_normal((T, K)) * s
    Q = np.random.standard_normal((N, K)) / np.sqrt(K) / s
    C_scale = (np.abs(C).reshape(T, K // B, B).max(axis=2) / 448.0).astype(np.float32)
    Q_scale = (np.abs(Q).reshape(N // B, B, K // B, B).max(axis=(1, 3)) / 448.0).astype(np.float32)
    C_bytes = e4m3fn_bytes(C / np.repeat(f64(C_scale), B, axis=1))
    Q_bytes = e4m3fn_bytes(Q / np.repeat(np.repeat(f64(Q_scale), B, axis=0), B, axis=1))
    return {"C_bytes": C_bytes, "C_scale": C_scale,
            "Q_bytes": Q_bytes, "Q_scale": Q_scale,
            "tau": bf(1 + 0.1 * np.random.standard_normal(N)),
            "b": bf(0.4 * np.random.standard_normal(T))}


def reference(C_bytes, C_scale, Q_bytes, Q_scale, tau, b):
    C = e4m3fn_values(C_bytes) * np.repeat(f64(C_scale), B, axis=1)
    Q = e4m3fn_values(Q_bytes) * np.repeat(np.repeat(f64(Q_scale), B, axis=0), B, axis=1)
    S = mxq(Q, 1, "e4m3") @ mxq(C, 1, "e4m3").T
    L = S * f64(tau)[:, None] + f64(b)[None, :]
    return L, L.max(axis=1)

@@ -1,0 +1,228 @@
+from contextlib import ExitStack
+
+import concourse.mybir as mybir
+from concourse.masks import make_identity
+
+N, T, K, B = 2048, 2048, 512, 128
+FLOPS = 2 * N * T * K
+
+F32 = mybir.dt.float32
+BF16 = mybir.dt.bfloat16
+U32 = mybir.dt.uint32
+U8 = mybir.dt.uint8
+FP8 = mybir.dt.float8_e4m3fn
+FP8X4 = mybir.dt.float8_e4m3fn_x4
+ALU = mybir.AluOpType
+ACT = mybir.ActivationFunctionType
+AX = mybir.AxisListType
+
+P = 128
+TG = 512
+NG = T // TG
+NR = N // P
+NJ = K // B
+
+
+def tile_absorbed_mla_cache_logits_d2_kernel(
+    tc, C_bytes, C_scale, Q_bytes, Q_scale, tau, b, out_0, out_1
+):
+    nc = tc.nc
+    with ExitStack() as ctx:
+        keep = ctx.enter_context(tc.tile_pool(name="keep", bufs=1))
+        wide = ctx.enter_context(tc.tile_pool(name="wide", bufs=3))
+        grp = ctx.enter_context(tc.tile_pool(name="grp", bufs=3))
+        outs = ctx.enter_context(tc.tile_pool(name="outs", bufs=8))
+        tps = ctx.enter_context(tc.psum_pool(name="tps", bufs=2))
+        acc_pool = ctx.enter_context(tc.psum_pool(name="accs", bufs=6))
+
+        cs = keep.tile([P, NG, 4 * NJ], F32, name="cs")
+        nc.scalar.dma_start(out=cs[:], in_=C_scale.rearrange("(g p c) j -> p g (c j)", p=P, c=4))
+        qs_all = keep.tile([P, NR * NJ], F32, name="qs_all")
+        nc.scalar.dma_start(out=qs_all[:], in_=Q_scale.rearrange("i j -> (i j)").partition_broadcast(P))
+        tau_b = keep.tile([P, NR], BF16, name="tau_b")
+        nc.scalar.dma_start(out=tau_b[:], in_=tau.rearrange("(p c) -> p c", c=NR))
+
+        c_view = C_bytes.rearrange("(g p c) k -> g p (c k)", p=P, c=4)
+        q_view = Q_bytes.rearrange("(p c) (j k) -> j p c k", c=NR, j=NJ)
+        cb = []
+        for g in range(NG):
+            cb.append(keep.tile([P, 4 * K], U8, name="cb%d" % g, align_bytes=64))
+        qb0 = keep.tile([P, NJ, 4 * B], U8, name="qb0", align_bytes=64)
+        qb1 = keep.tile([P, NJ, 12 * B], U8, name="qb1", align_bytes=64)
+        b_sb = keep.tile([P, T], BF16, name="b_sb")
+        nc.sync.dma_start(out=cb[0][:], in_=c_view[0])
+        for j in range(NJ):
+            nc.sync.dma_start(out=qb0[:, j, :].rearrange("p (c k) -> p c k", c=4), in_=q_view[j][:, 0:4, :])
+        nc.sync.dma_start(out=cb[1][:], in_=c_view[1])
+        nc.sync.dma_start(out=b_sb[:], in_=b.partition_broadcast(P))
+        for g in range(2, NG):
+            nc.sync.dma_start(out=cb[g][:], in_=c_view[g])
+        for j in range(NJ):
+            nc.sync.dma_start(out=qb1[:, j, :].rearrange("p (c k) -> p c k", c=12), in_=q_view[j][:, 4:16, :])
+
+        ident = keep.tile([P, P], F32, name="ident")
+        make_identity(nc, ident[:])
+        mask = keep.tile([P, NR], F32, name="mask")
+        nc.gpsimd.memset(mask[:], 1.0)
+        nc.gpsimd.affine_select(
+            out=mask[:], in_=mask[:], pattern=[[-8, NR]], compare_op=ALU.is_ge, fill=0.0, base=0, channel_multiplier=1
+        )
+        nc.gpsimd.affine_select(
+            out=mask[:], in_=mask[:], pattern=[[8, NR]], compare_op=ALU.is_ge, fill=0.0, base=7, channel_multiplier=-1
+        )
+        qs_m = keep.tile([P, NJ, NR], F32, name="qs_m")
+        nc.vector.tensor_tensor(
+            out=qs_m[:],
+            in0=qs_all[:].rearrange("p (i j) -> p j i", j=NJ),
+            in1=mask[:].unsqueeze(1).to_broadcast([P, NJ, NR]),
+            op=ALU.mult,
+        )
+        qs = keep.tile([P, NJ], F32, name="qs")
+        nc.vector.tensor_reduce(out=qs[:], in_=qs_m[:], axis=AX.X, op=ALU.add)
+        tau_f = keep.tile([P, NR], F32, name="tau_f")
+        nc.vector.tensor_copy(out=tau_f[:], in_=tau_b[:])
+
+        c_codes, c_scales, q_codes, q_scales = [], [], [], []
+        for g in range(NG):
+            c_codes.append(keep.tile([P, TG], U32, name="cc%d" % g, align_bytes=64))
+            c_scales.append(keep.tile([P, TG], U8, name="csc%d" % g, align_bytes=64))
+        for h in range(NR // 2):
+            q_codes.append(keep.tile([P, 2 * P], U32, name="qc%d" % h, align_bytes=64))
+            q_scales.append(keep.tile([P, 2 * P], U8, name="qsc%d" % h, align_bytes=64))
+        mx = keep.tile([P, NR], F32, name="mx")
+
+        def widen(dst, src, col, on_vector):
+            if on_vector:
+                nc.vector.tensor_scalar(out=dst, in0=src, scalar1=col, scalar2=None, op0=ALU.mult)
+            else:
+                nc.scalar.activation(out=dst, in_=src, func=ACT.Copy, scale=col)
+
+        def turn(words, pair, first):
+            bank = tps.tile([P, 4, P], F32, name="bank")
+            for c in range(2):
+                for u in range(2):
+                    w0 = 256 * (first + c)
+                    nc.tensor.transpose(bank[:, 2 * c + u, :], words[:, w0 + u : w0 + 256 : 2], ident[:])
+            return bank
+
+        def copy_out(dst, src, on_vector):
+            if on_vector:
+                nc.vector.tensor_copy(out=dst, in_=src)
+            else:
+                nc.scalar.copy(out=dst, in_=src)
+
+        def prep_c(g, nv, evac_v):
+            w = wide.tile([P, 4 * K], BF16, name="w", align_bytes=64)
+            gt = grp.tile([P, TG, 4], BF16, name="gt", align_bytes=64)
+            for c in range(4):
+                for j in range(NJ):
+                    i = 4 * c + j
+                    widen(
+                        w[:, B * i : B * (i + 1)],
+                        cb[g][:, B * i : B * (i + 1)].bitcast(FP8),
+                        cs[:, g, i : i + 1],
+                        i % 16 in nv,
+                    )
+            gw = gt[:].rearrange("p n t -> p (n t)").bitcast(F32).rearrange("p (r q) -> p r q", q=8)
+            for h in range(2):
+                bank = turn(w[:].bitcast(F32), h, 2 * h)
+                copy_out(gw[:, :, 4 * h : 4 * h + 4], bank[:].rearrange("p q r -> p r q"), evac_v[h])
+            nc.vector.quantize_mx(
+                out=c_codes[g][:].bitcast(FP8X4), scales=c_scales[g][:], in_=gt[:].rearrange("p n t -> p (n t)")
+            )
+
+        def prep_q(q, evac_v):
+            w = wide.tile([P, 4 * K], BF16, name="w", align_bytes=64)
+            src, off = (qb0, 0) if q == 0 else (qb1, 4 * B * (q - 1))
+            for j in range(NJ):
+                nc.vector.tensor_scalar(
+                    out=w[:].rearrange("p (c k) -> p c k", c=4)[:, :, B * j : B * (j + 1)],
+                    in0=src[:, j, off : off + 4 * B].bitcast(FP8).rearrange("p (c k) -> p c k", c=4),
+                    scalar1=qs[:, j : j + 1],
+                    scalar2=None,
+                    op0=ALU.mult,
+                )
+            for h in range(2):
+                gt = grp.tile([P, 2 * P, 4], BF16, name="gq", align_bytes=64)
+                gf = gt[:].rearrange("p n t -> p (n t)")
+                bank = turn(w[:].bitcast(F32), 0, 2 * h)
+                copy_out(
+                    gf.bitcast(F32).rearrange("p (c r u) -> p c r u", c=2, u=2),
+                    bank[:].rearrange("p (c u) r -> p c r u", u=2),
+                    evac_v[h],
+                )
+                i = 2 * q + h
+                nc.vector.quantize_mx(out=q_codes[i][:].bitcast(FP8X4), scales=q_scales[i][:], in_=gf)
+
+        out_view = out_0.rearrange("(p c) j -> c p j", c=NR)
+        tiles = {}
+
+        def mm(c, g):
+            acc = acc_pool.tile([P, TG], F32, name="acc")
+            cols = slice(P * (c % 2), P * (c % 2 + 1))
+            nc.tensor.matmul_mx(
+                out=acc[:],
+                lhsT=q_codes[c // 2][:, cols].bitcast(FP8X4),
+                lhsT_scale=q_scales[c // 2][:, cols],
+                rhs=c_codes[g][:].bitcast(FP8X4),
+                rhs_scale=c_scales[g][:],
+                start=True,
+                stop=True,
+            )
+            return acc
+
+        def bank_a(c, g):
+            acc = mm(c, g)
+            cols = slice(TG * g, TG * (g + 1))
+            nc.vector.scalar_tensor_tensor(
+                out=tiles[c][:, cols], in0=acc[:], scalar=tau_f[:, c : c + 1], in1=b_sb[:, cols], op0=ALU.mult, op1=ALU.add
+            )
+
+        def bank_s(c, g):
+            acc = mm(c, g)
+            cols = slice(TG * g, TG * (g + 1))
+            nc.scalar.activation(out=tiles[c][:, cols], in_=acc[:], func=ACT.Copy, scale=tau_f[:, c : c + 1])
+
+        def add_b(c, g0, n):
+            cols = slice(TG * g0, TG * (g0 + n))
+            nc.gpsimd.tensor_tensor(out=tiles[c][:, cols], in0=tiles[c][:, cols], in1=b_sb[:, cols], op=ALU.add)
+
+        def store(c, g0, n):
+            cols = slice(TG * g0, TG * (g0 + n))
+            nc.sync.dma_start(out=out_view[c][:, cols], in_=tiles[c][:, cols])
+
+        def row_max(c):
+            nc.vector.tensor_reduce(out=mx[:, c : c + 1], in_=tiles[c][:], axis=AX.X, op=ALU.max)
+
+        prep_c(0, (2, 5, 8, 11, 13, 15), (True, False))
+        prep_q(0, (True, False))
+        for c in range(4):
+            tiles[c] = outs.tile([P, T], F32, name="L")
+        for g in range(4):
+            if g < 3:
+                prep_c(g + 1, (), (False, False))
+            else:
+                prep_q(1, (False, False))
+            for c in range(4):
+                if (c + g) % 2 == 0:
+                    bank_a(c, g)
+                else:
+                    bank_s(c, g)
+                    add_b(c, g, 1)
+                store(c, g, 1)
+        for c in range(4):
+            row_max(c)
+        for c in range(4, NR):
+            if c % 4 == 1 and c // 4 + 1 < NR // 4:
+                prep_q(c // 4 + 1, (False, False))
+            tiles[c] = outs.tile([P, T], F32, name="L")
+            na = 1
+            for g in range(na, 4):
+                bank_s(c, g)
+            add_b(c, na, 4 - na)
+            for g in range(na):
+                bank_a(c, g)
+            store(c, 0, na)
+            store(c, na, 4 - na)
+            row_max(c)
+        nc.sync.dma_start(out=out_1.rearrange("(p c) -> p c", c=NR), in_=mx[:])

@@ -21,6 +21,7 @@ TG = 512
 NG = T // TG
 NR = N // P
 NJ = K // B
+NPB = 1
 
 
 def tile_absorbed_mla_cache_logits_d2_kernel(
@@ -31,9 +32,10 @@ def tile_absorbed_mla_cache_logits_d2_kernel(
         keep = ctx.enter_context(tc.tile_pool(name="keep", bufs=1))
         wide = ctx.enter_context(tc.tile_pool(name="wide", bufs=3))
         grp = ctx.enter_context(tc.tile_pool(name="grp", bufs=3))
-        outs = ctx.enter_context(tc.tile_pool(name="outs", bufs=8))
+        outs = ctx.enter_context(tc.tile_pool(name="outs", bufs=1))
         tps = ctx.enter_context(tc.psum_pool(name="tps", bufs=2))
-        acc_pool = ctx.enter_context(tc.psum_pool(name="accs", bufs=6))
+        acc_pool = ctx.enter_context(tc.psum_pool(name="accs", bufs=5))
+        xs_pool = ctx.enter_context(tc.tile_pool(name="xs", bufs=2))
 
         cs = keep.tile([P, NG, 4 * NJ], F32, name="cs")
         nc.scalar.dma_start(out=cs[:], in_=C_scale.rearrange("(g p c) j -> p g (c j)", p=P, c=4))
@@ -86,10 +88,14 @@ def tile_absorbed_mla_cache_logits_d2_kernel(
         for g in range(NG):
             c_codes.append(keep.tile([P, TG], U32, name="cc%d" % g, align_bytes=64))
             c_scales.append(keep.tile([P, TG], U8, name="csc%d" % g, align_bytes=64))
-        for h in range(NR // 2):
-            q_codes.append(keep.tile([P, 2 * P], U32, name="qc%d" % h, align_bytes=64))
-            q_scales.append(keep.tile([P, 2 * P], U8, name="qsc%d" % h, align_bytes=64))
+        for q in range(NR // 4):
+            q_codes.append(keep.tile([P, 4 * P], U32, name="qc%d" % q, align_bytes=64))
+            q_scales.append(keep.tile([P, 4 * P], U8, name="qsc%d" % q, align_bytes=64))
         mx = keep.tile([P, NR], F32, name="mx")
+        mx2 = keep.tile([P, NR, 2], F32, name="mx2")
+        first_row = keep.tile([P, P], BF16, name="first_row")
+        nc.gpsimd.memset(first_row[:], 0.0)
+        nc.gpsimd.memset(first_row[0:1, :], 1.0)
 
         def widen(dst, src, col, on_vector):
             if on_vector:
@@ -111,118 +117,212 @@ def tile_absorbed_mla_cache_logits_d2_kernel(
             else:
                 nc.scalar.copy(out=dst, in_=src)
 
-        def prep_c(g, nv, evac_v):
-            w = wide.tile([P, 4 * K], BF16, name="w", align_bytes=64)
-            gt = grp.tile([P, TG, 4], BF16, name="gt", align_bytes=64)
-            for c in range(4):
-                for j in range(NJ):
-                    i = 4 * c + j
-                    widen(
-                        w[:, B * i : B * (i + 1)],
-                        cb[g][:, B * i : B * (i + 1)].bitcast(FP8),
-                        cs[:, g, i : i + 1],
-                        i % 16 in nv,
-                    )
-            gw = gt[:].rearrange("p n t -> p (n t)").bitcast(F32).rearrange("p (r q) -> p r q", q=8)
-            for h in range(2):
-                bank = turn(w[:].bitcast(F32), h, 2 * h)
-                copy_out(gw[:, :, 4 * h : 4 * h + 4], bank[:].rearrange("p q r -> p r q"), evac_v[h])
+        wide_c, gath_c, wide_q, gath_q = {}, {}, {}, {}
+
+        def widen_c(g, pieces, on_vector):
+            if g not in wide_c:
+                wide_c[g] = wide.tile([P, 4 * K], BF16, name="w", align_bytes=64)
+                gath_c[g] = grp.tile([P, TG, 4], BF16, name="gt", align_bytes=64)
+            for i in pieces:
+                widen(
+                    wide_c[g][:, B * i : B * (i + 1)],
+                    cb[g][:, B * i : B * (i + 1)].bitcast(FP8),
+                    cs[:, g, i : i + 1],
+                    on_vector,
+                )
+
+        def turn_c(g, h, on_vector):
+            gw = gath_c[g][:].rearrange("p n t -> p (n t)").bitcast(F32).rearrange("p (r q) -> p r q", q=8)
+            bank = turn(wide_c[g][:].bitcast(F32), h, 2 * h)
+            copy_out(gw[:, :, 4 * h : 4 * h + 4], bank[:].rearrange("p q r -> p r q"), on_vector)
+
+        def quantize_c(g):
             nc.vector.quantize_mx(
-                out=c_codes[g][:].bitcast(FP8X4), scales=c_scales[g][:], in_=gt[:].rearrange("p n t -> p (n t)")
+                out=c_codes[g][:].bitcast(FP8X4),
+                scales=c_scales[g][:],
+                in_=gath_c[g][:].rearrange("p n t -> p (n t)"),
             )
 
-        def prep_q(q, evac_v):
-            w = wide.tile([P, 4 * K], BF16, name="w", align_bytes=64)
+        def widen_q(q, c, js, on_vector):
+            if q not in wide_q:
+                wide_q[q] = wide.tile([P, 4 * K], BF16, name="w", align_bytes=64)
             src, off = (qb0, 0) if q == 0 else (qb1, 4 * B * (q - 1))
-            for j in range(NJ):
-                nc.vector.tensor_scalar(
-                    out=w[:].rearrange("p (c k) -> p c k", c=4)[:, :, B * j : B * (j + 1)],
-                    in0=src[:, j, off : off + 4 * B].bitcast(FP8).rearrange("p (c k) -> p c k", c=4),
-                    scalar1=qs[:, j : j + 1],
-                    scalar2=None,
-                    op0=ALU.mult,
-                )
-            for h in range(2):
-                gt = grp.tile([P, 2 * P, 4], BF16, name="gq", align_bytes=64)
-                gf = gt[:].rearrange("p n t -> p (n t)")
-                bank = turn(w[:].bitcast(F32), 0, 2 * h)
-                copy_out(
-                    gf.bitcast(F32).rearrange("p (c r u) -> p c r u", c=2, u=2),
-                    bank[:].rearrange("p (c u) r -> p c r u", u=2),
-                    evac_v[h],
-                )
-                i = 2 * q + h
-                nc.vector.quantize_mx(out=q_codes[i][:].bitcast(FP8X4), scales=q_scales[i][:], in_=gf)
+            for j in js:
+                if on_vector:
+                    nc.vector.tensor_scalar(
+                        out=wide_q[q][:].rearrange("p (c k) -> p c k", c=4)[:, :, B * j : B * (j + 1)],
+                        in0=src[:, j, off : off + 4 * B].bitcast(FP8).rearrange("p (c k) -> p c k", c=4),
+                        scalar1=qs[:, j : j + 1],
+                        scalar2=None,
+                        op0=ALU.mult,
+                    )
+                else:
+                    nc.scalar.activation(
+                        out=wide_q[q][:, K * c + B * j : K * c + B * (j + 1)],
+                        in_=src[:, j, off + B * c : off + B * (c + 1)].bitcast(FP8),
+                        func=ACT.Copy,
+                        scale=qs[:, j : j + 1],
+                    )
+
+        def turn_q(q, h, on_vector):
+            if q not in gath_q:
+                gath_q[q] = grp.tile([P, TG, 4], BF16, name="gt", align_bytes=64)
+            gf = gath_q[q][:, 2 * P * h : 2 * P * (h + 1), :].rearrange("p n t -> p (n t)")
+            bank = turn(wide_q[q][:].bitcast(F32), 0, 2 * h)
+            copy_out(
+                gf.bitcast(F32).rearrange("p (c r u) -> p c r u", c=2, u=2),
+                bank[:].rearrange("p (c u) r -> p c r u", u=2),
+                on_vector,
+            )
+
+        def quantize_q(q):
+            nc.vector.quantize_mx(
+                out=q_codes[q][:].bitcast(FP8X4),
+                scales=q_scales[q][:],
+                in_=gath_q[q][:].rearrange("p n t -> p (n t)"),
+            )
 
         out_view = out_0.rearrange("(p c) j -> c p j", c=NR)
-        tiles = {}
+        tiles, accs = {}, {}
 
         def mm(c, g):
             acc = acc_pool.tile([P, TG], F32, name="acc")
-            cols = slice(P * (c % 2), P * (c % 2 + 1))
+            cols = slice(P * (c % 4), P * (c % 4 + 1))
             nc.tensor.matmul_mx(
                 out=acc[:],
-                lhsT=q_codes[c // 2][:, cols].bitcast(FP8X4),
-                lhsT_scale=q_scales[c // 2][:, cols],
+                lhsT=q_codes[c // 4][:, cols].bitcast(FP8X4),
+                lhsT_scale=q_scales[c // 4][:, cols],
                 rhs=c_codes[g][:].bitcast(FP8X4),
                 rhs_scale=c_scales[g][:],
                 start=True,
                 stop=True,
             )
-            return acc
+            accs[c, g] = acc
 
         def bank_a(c, g):
-            acc = mm(c, g)
             cols = slice(TG * g, TG * (g + 1))
             nc.vector.scalar_tensor_tensor(
-                out=tiles[c][:, cols], in0=acc[:], scalar=tau_f[:, c : c + 1], in1=b_sb[:, cols], op0=ALU.mult, op1=ALU.add
+                out=tiles[c][:, cols],
+                in0=accs[c, g][:],
+                scalar=tau_f[:, c : c + 1],
+                in1=b_sb[:, cols],
+                op0=ALU.mult,
+                op1=ALU.add,
             )
 
         def bank_s(c, g):
-            acc = mm(c, g)
             cols = slice(TG * g, TG * (g + 1))
-            nc.scalar.activation(out=tiles[c][:, cols], in_=acc[:], func=ACT.Copy, scale=tau_f[:, c : c + 1])
+            nc.scalar.activation(out=tiles[c][:, cols], in_=accs[c, g][:], func=ACT.Copy, scale=tau_f[:, c : c + 1])
 
         def add_b(c, g0, n):
             cols = slice(TG * g0, TG * (g0 + n))
             nc.gpsimd.tensor_tensor(out=tiles[c][:, cols], in0=tiles[c][:, cols], in1=b_sb[:, cols], op=ALU.add)
 
+        def bank_p(c, g):
+            cols = slice(TG * g, TG * (g + 1))
+            x = xs_pool.tile([P, TG], F32, name="x")
+            nc.scalar.activation(out=x[:], in_=accs[c, g][:], func=ACT.Copy, scale=tau_f[:, c : c + 1])
+            acc = acc_pool.tile([P, TG], F32, name="acc_p", bufs=NPB)
+            nc.tensor.matmul(acc[:], lhsT=ident[:], rhs=x[:], start=True, stop=False)
+            nc.tensor.matmul(acc[:], lhsT=first_row[:], rhs=b_sb[:, cols], start=False, stop=True)
+            accs[c, g] = acc
+
+        def leave_p(c, g):
+            cols = slice(TG * g, TG * (g + 1))
+            nc.vector.tensor_scalar(
+                out=tiles[c][:, cols],
+                in0=accs[c, g][:],
+                scalar1=1.0,
+                scalar2=None,
+                op0=ALU.mult,
+                op1=ALU.max,
+                accum_out=mx2[:, c, 1:2],
+            )
+
         def store(c, g0, n):
             cols = slice(TG * g0, TG * (g0 + n))
             nc.sync.dma_start(out=out_view[c][:, cols], in_=tiles[c][:, cols])
 
-        def row_max(c):
-            nc.vector.tensor_reduce(out=mx[:, c : c + 1], in_=tiles[c][:], axis=AX.X, op=ALU.max)
+        def row_max(c, g0, n, k):
+            cols = slice(TG * g0, TG * (g0 + n))
+            nc.vector.tensor_reduce(out=mx2[:, c, k : k + 1], in_=tiles[c][:, cols], axis=AX.X, op=ALU.max)
 
-        prep_c(0, (2, 5, 8, 11, 13, 15), (True, False))
-        prep_q(0, (True, False))
-        for c in range(4):
-            tiles[c] = outs.tile([P, T], F32, name="L")
+        for c in range(NR):
+            tiles[c] = outs.tile([P, T], F32, name="L%d" % c)
+        ON_S, ON_V = (0, 1, 2, 3, 8, 9, 10, 11), (4, 5, 6, 7, 12, 13, 14, 15)
+        KIND = ['AAAA', 'AAAB', 'AAAB', 'AABB'] + ['PBBB' if c % 3 == 2 else 'PABB' for c in range(4, 16)]
+        LEAD = 3
+
+        widen_c(0, (0, 1, 2, 3, 8, 9, 10, 11), False)
+        widen_c(0, (4, 5, 6, 7, 12, 13, 14, 15), True)
+        turn_c(0, 0, False)
+        widen_q(0, 0, range(4), True)
+        turn_c(0, 1, True)
+        for g in range(1, 4):
+            widen_c(g, ON_S, False)
+            widen_c(g, ON_V, True)
+            if g == 1:
+                turn_q(0, 0, False)
+                turn_q(0, 1, False)
+            quantize_c(g - 1)
+            if g == 1:
+                quantize_q(0)
+            turn_c(g, 0, False)
+            turn_c(g, 1, g == 3)
+        quantize_c(3)
+
+        def prep(r):
+            q, k = r // 4 + 1, r % 4
+            if r < 0 or q > 3:
+                return
+            widen_q(q, k, range(4), False)
+            if k == 2:
+                turn_q(q, 0, False)
+
+        def prep_end(r):
+            q, k = r // 4 + 1, r % 4
+            if r >= 0 and q <= 3 and k == 3:
+                turn_q(q, 1, False)
+                quantize_q(q)
+
         for g in range(4):
-            if g < 3:
-                prep_c(g + 1, (), (False, False))
-            else:
-                prep_q(1, (False, False))
-            for c in range(4):
-                if (c + g) % 2 == 0:
-                    bank_a(c, g)
-                else:
+            mm(0, g)
+        for r in range(LEAD):
+            prep(r)
+        for c in range(NR + 2):
+            if c < NR:
+                if KIND[c][0] == "P":
+                    bank_p(c, 0)
+            if c < NR:
+                nb = KIND[c].count("B")
+                for g in range(4 - nb, 4):
                     bank_s(c, g)
-                    add_b(c, g, 1)
-                store(c, g, 1)
-        for c in range(4):
-            row_max(c)
-        for c in range(4, NR):
-            if c % 4 == 1 and c // 4 + 1 < NR // 4:
-                prep_q(c // 4 + 1, (False, False))
-            tiles[c] = outs.tile([P, T], F32, name="L")
-            na = 1
-            for g in range(na, 4):
-                bank_s(c, g)
-            add_b(c, na, 4 - na)
-            for g in range(na):
-                bank_a(c, g)
-            store(c, 0, na)
-            store(c, na, 4 - na)
-            row_max(c)
+                if nb:
+                    add_b(c, 4 - nb, nb)
+                prep(c + LEAD)
+                prep_end(c + LEAD - 1)
+                if c + 1 < NR:
+                    for g in range(4):
+                        mm(c + 1, g)
+            if 1 <= c <= NR and KIND[c - 1][0] == "P":
+                leave_p(c - 1, 0)
+                store(c - 1, 0, KIND[c - 1].count("A") + 1)
+            if c < NR:
+                na = KIND[c].count("A")
+                for g in range(4):
+                    if KIND[c][g] == "A":
+                        bank_a(c, g)
+                if KIND[c][0] == "A":
+                    store(c, 0, na)
+            if 1 <= c <= NR:
+                nb = KIND[c - 1].count("B")
+                if nb:
+                    store(c - 1, 4 - nb, nb)
+            if c >= 2:
+                if KIND[c - 2][0] == "P":
+                    row_max(c - 2, 1, 3, 0)
+                else:
+                    row_max(c - 2, 0, 2, 0)
+                    row_max(c - 2, 2, 2, 1)
+        nc.vector.tensor_reduce(out=mx[:], in_=mx2[:], axis=AX.X, op=ALU.max)
         nc.sync.dma_start(out=out_1.rearrange("(p c) -> p c", c=NR), in_=mx[:])

@@ -55,10 +55,11 @@ def tile_absorbed_mla_cache_logits_d2_kernel(
         nc.sync.dma_start(out=cb[0][:], in_=c_view[0])
         for j in range(NJ):
             nc.sync.dma_start(out=qb0[:, j, :].rearrange("p (c k) -> p c k", c=4), in_=q_view[j][:, 0:4, :])
-        nc.sync.dma_start(out=cb[1][:], in_=c_view[1])
-        nc.sync.dma_start(out=b_sb[:], in_=b.partition_broadcast(P))
-        for g in range(2, NG):
+        for g in range(1, NG):
             nc.sync.dma_start(out=cb[g][:], in_=c_view[g])
+        for h in range(2):
+            cols = slice(T // 2 * h, T // 2 * (h + 1))
+            nc.sync.dma_start(out=b_sb[:, cols], in_=b[cols].partition_broadcast(P))
         for j in range(NJ):
             nc.sync.dma_start(out=qb1[:, j, :].rearrange("p (c k) -> p c k", c=12), in_=q_view[j][:, 4:16, :])
 
@@ -250,8 +251,9 @@ def tile_absorbed_mla_cache_logits_d2_kernel(
         for c in range(NR):
             tiles[c] = outs.tile([P, T], F32, name="L%d" % c)
         ON_S, ON_V = (0, 1, 2, 3, 8, 9, 10, 11), (4, 5, 6, 7, 12, 13, 14, 15)
-        KIND = ['AAAA', 'AAAB', 'AAAB', 'AABB'] + ['PBBB' if c % 3 == 2 else 'PABB' for c in range(4, 16)]
+        KIND = ['AAAA', 'AAAB', 'AABB', 'AABB'] + ['PAAA' if c in (5, 9) else 'PBBB' if c in (6, 13, 14) else 'PABB' for c in range(4, 16)]
         LEAD = 3
+        LAG = 2
 
         widen_c(0, (0, 1, 2, 3, 8, 9, 10, 11), False)
         widen_c(0, (4, 5, 6, 7, 12, 13, 14, 15), True)
@@ -289,7 +291,7 @@ def tile_absorbed_mla_cache_logits_d2_kernel(
             mm(0, g)
         for r in range(LEAD):
             prep(r)
-        for c in range(NR + 2):
+        for c in range(NR + LAG):
             if c < NR:
                 if KIND[c][0] == "P":
                     bank_p(c, 0)
@@ -318,11 +320,11 @@ def tile_absorbed_mla_cache_logits_d2_kernel(
                 nb = KIND[c - 1].count("B")
                 if nb:
                     store(c - 1, 4 - nb, nb)
-            if c >= 2:
-                if KIND[c - 2][0] == "P":
-                    row_max(c - 2, 1, 3, 0)
+            if LAG <= c < NR + LAG:
+                if KIND[c - LAG][0] == "P":
+                    row_max(c - LAG, 1, 3, 0)
                 else:
-                    row_max(c - 2, 0, 2, 0)
-                    row_max(c - 2, 2, 2, 1)
+                    row_max(c - LAG, 0, 2, 0)
+                    row_max(c - LAG, 2, 2, 1)
         nc.vector.tensor_reduce(out=mx[:], in_=mx2[:], axis=AX.X, op=ALU.max)
         nc.sync.dma_start(out=out_1.rearrange("(p c) -> p c", c=NR), in_=mx[:])

@@ -33,8 +33,7 @@ def tile_absorbed_mla_cache_logits_d2_kernel(
         wide = ctx.enter_context(tc.tile_pool(name="wide", bufs=3))
         grp = ctx.enter_context(tc.tile_pool(name="grp", bufs=3))
         outs = ctx.enter_context(tc.tile_pool(name="outs", bufs=1))
-        tps = ctx.enter_context(tc.psum_pool(name="tps", bufs=2))
-        acc_pool = ctx.enter_context(tc.psum_pool(name="accs", bufs=5))
+        acc_pool = ctx.enter_context(tc.psum_pool(name="accs", bufs=7))
         xs_pool = ctx.enter_context(tc.tile_pool(name="xs", bufs=2))
 
         cs = keep.tile([P, NG, 4 * NJ], F32, name="cs")
@@ -105,7 +104,7 @@ def tile_absorbed_mla_cache_logits_d2_kernel(
                 nc.scalar.activation(out=dst, in_=src, func=ACT.Copy, scale=col)
 
         def turn(words, pair, first):
-            bank = tps.tile([P, 4, P], F32, name="bank")
+            bank = acc_pool.tile([P, 4, P], F32, name="bank", tag="bank")
             for c in range(2):
                 for u in range(2):
                     w0 = 256 * (first + c)
@@ -187,7 +186,7 @@ def tile_absorbed_mla_cache_logits_d2_kernel(
         tiles, accs = {}, {}
 
         def mm(c, g):
-            acc = acc_pool.tile([P, TG], F32, name="acc")
+            acc = acc_pool.tile([P, TG], F32, name="acc", tag="bank")
             cols = slice(P * (c % 4), P * (c % 4 + 1))
             nc.tensor.matmul_mx(
                 out=acc[:],
@@ -251,71 +250,98 @@ def tile_absorbed_mla_cache_logits_d2_kernel(
         for c in range(NR):
             tiles[c] = outs.tile([P, T], F32, name="L%d" % c)
         ON_S, ON_V = (0, 1, 2, 3, 8, 9, 10, 11), (4, 5, 6, 7, 12, 13, 14, 15)
-        KIND = ['AAAA', 'AAAB', 'AABB', 'AABB'] + ['PAAA' if c in (5, 9) else 'PBBB' if c in (6, 13, 14) else 'PABB' for c in range(4, 16)]
+        KIND = ['AAAB', 'AAAB', 'AABB', 'AABB', 'PABB', 'PABB', 'PAAB', 'ABBB', 'PABB', 'PABB', 'PBBB', 'PABB', 'PABB', 'PABB', 'PBBB', 'PABB']
         LEAD = 3
         LAG = 2
 
         widen_c(0, (0, 1, 2, 3, 8, 9, 10, 11), False)
         widen_c(0, (4, 5, 6, 7, 12, 13, 14, 15), True)
-        turn_c(0, 0, False)
         widen_q(0, 0, range(4), True)
+        widen_c(1, ON_S, False)
+        widen_c(1, ON_V, True)
+        turn_c(0, 0, False)
         turn_c(0, 1, True)
-        for g in range(1, 4):
-            widen_c(g, ON_S, False)
-            widen_c(g, ON_V, True)
-            if g == 1:
-                turn_q(0, 0, False)
-                turn_q(0, 1, False)
-            quantize_c(g - 1)
-            if g == 1:
-                quantize_q(0)
-            turn_c(g, 0, False)
-            turn_c(g, 1, g == 3)
-        quantize_c(3)
+        turn_q(0, 0, False)
+        turn_q(0, 1, False)
+        widen_c(2, ON_S, False)
+        widen_c(2, ON_V, True)
+        quantize_c(0)
+        quantize_q(0)
+        turn_c(1, 0, False)
+        turn_c(1, 1, False)
+        for c in range(4):
+            mm(c, 0)
+        widen_c(3, ON_S, False)
+        widen_c(3, ON_V, True)
+        bank_a(0, 0)
+        bank_a(1, 0)
+        quantize_c(1)
+        turn_c(2, 0, False)
+        turn_c(2, 1, False)
+        bank_a(2, 0)
+        bank_a(3, 0)
+        for c in range(4):
+            store(c, 0, 1)
 
         def prep(r):
             q, k = r // 4 + 1, r % 4
             if r < 0 or q > 3:
                 return
             widen_q(q, k, range(4), False)
-            if k == 2:
+
+        def prep_turn(r):
+            q, k = r // 4 + 1, r % 4
+            if r >= 0 and q <= 3 and k == 3:
                 turn_q(q, 0, False)
+                turn_q(q, 1, False)
 
         def prep_end(r):
             q, k = r // 4 + 1, r % 4
             if r >= 0 and q <= 3 and k == 3:
-                turn_q(q, 1, False)
                 quantize_q(q)
 
-        for g in range(4):
-            mm(0, g)
+        for c in range(2):
+            mm(c, 1)
+        turn_c(3, 0, False)
+        turn_c(3, 1, False)
+        quantize_c(2)
+        for c in range(2):
+            bank_a(c, 1)
+            store(c, 1, 1)
         for r in range(LEAD):
             prep(r)
+        quantize_c(3)
+        done = {(0, 0), (1, 0), (2, 0), (3, 0), (0, 1), (1, 1)}
+
+        def mms(c):
+            for g in range(4):
+                if (c, g) not in done:
+                    mm(c, g)
+
+        mms(0)
         for c in range(NR + LAG):
             if c < NR:
                 if KIND[c][0] == "P":
                     bank_p(c, 0)
-            if c < NR:
                 nb = KIND[c].count("B")
                 for g in range(4 - nb, 4):
                     bank_s(c, g)
                 if nb:
                     add_b(c, 4 - nb, nb)
                 prep(c + LEAD)
-                prep_end(c + LEAD - 1)
+                prep_turn(c + LEAD - 1)
+                prep_end(c + LEAD - 2)
                 if c + 1 < NR:
-                    for g in range(4):
-                        mm(c + 1, g)
+                    mms(c + 1)
             if 1 <= c <= NR and KIND[c - 1][0] == "P":
                 leave_p(c - 1, 0)
                 store(c - 1, 0, KIND[c - 1].count("A") + 1)
             if c < NR:
-                na = KIND[c].count("A")
                 for g in range(4):
-                    if KIND[c][g] == "A":
+                    if KIND[c][g] == "A" and (c, g) not in done:
                         bank_a(c, g)
-                if KIND[c][0] == "A":
-                    store(c, 0, na)
+                        if KIND[c][0] == "A":
+                            store(c, g, 1)
             if 1 <= c <= NR:
                 nb = KIND[c - 1].count("B")
                 if nb:

@@ -37,50 +37,51 @@ def tile_absorbed_mla_cache_logits_d2_kernel(
         xs_pool = ctx.enter_context(tc.tile_pool(name="xs", bufs=2))
 
         cs = keep.tile([P, NG, 4 * NJ], F32, name="cs")
-        nc.scalar.dma_start(out=cs[:], in_=C_scale.rearrange("(g p c) j -> p g (c j)", p=P, c=4))
-        qs_all = keep.tile([P, NR * NJ], F32, name="qs_all")
-        nc.scalar.dma_start(out=qs_all[:], in_=Q_scale.rearrange("i j -> (i j)").partition_broadcast(P))
+        cs_view = C_scale.rearrange("(g p c) j -> p g (c j)", p=P, c=4)
+        nc.scalar.dma_start(out=cs[:, 0:1, :], in_=cs_view[:, 0:1, :])
+        qs_in = keep.tile([P, NJ], F32, name="qs_in")
+        nc.vector.memset(qs_in[:], 0.0)
+        nc.scalar.dma_start(out=qs_in[0:NR, :], in_=Q_scale)
+        nc.scalar.dma_start(out=cs[:, 1:NG, :], in_=cs_view[:, 1:NG, :])
         tau_b = keep.tile([P, NR], BF16, name="tau_b")
         nc.scalar.dma_start(out=tau_b[:], in_=tau.rearrange("(p c) -> p c", c=NR))
 
         c_view = C_bytes.rearrange("(g p c) k -> g p (c k)", p=P, c=4)
-        q_view = Q_bytes.rearrange("(p c) (j k) -> j p c k", c=NR, j=NJ)
-        cb = []
+        q_view = Q_bytes.rearrange("(p c) k -> p (c k)", c=NR)
+        cb, qb = [], []
         for g in range(NG):
             cb.append(keep.tile([P, 4 * K], U8, name="cb%d" % g, align_bytes=64))
-        qb0 = keep.tile([P, NJ, 4 * B], U8, name="qb0", align_bytes=64)
-        qb1 = keep.tile([P, NJ, 12 * B], U8, name="qb1", align_bytes=64)
+            qb.append(keep.tile([P, 4 * K], U8, name="qb%d" % g, align_bytes=64))
         b_sb = keep.tile([P, T], BF16, name="b_sb")
+        b_row = keep.tile([P, TG], BF16, name="b_row")
+        nc.vector.memset(b_row[:], 0.0)
+        nc.scalar.dma_start(out=b_row[0:1, :], in_=b[0:TG].unsqueeze(0))
         nc.sync.dma_start(out=cb[0][:], in_=c_view[0])
-        for j in range(NJ):
-            nc.sync.dma_start(out=qb0[:, j, :].rearrange("p (c k) -> p c k", c=4), in_=q_view[j][:, 0:4, :])
+        nc.sync.dma_start(out=qb[0][:], in_=q_view[:, 0 : 4 * K])
         for g in range(1, NG):
             nc.sync.dma_start(out=cb[g][:], in_=c_view[g])
-        for h in range(2):
-            cols = slice(T // 2 * h, T // 2 * (h + 1))
-            nc.sync.dma_start(out=b_sb[:, cols], in_=b[cols].partition_broadcast(P))
-        for j in range(NJ):
-            nc.sync.dma_start(out=qb1[:, j, :].rearrange("p (c k) -> p c k", c=12), in_=q_view[j][:, 4:16, :])
+        for q in range(1, NG):
+            nc.sync.dma_start(out=qb[q][:], in_=q_view[:, 4 * K * q : 4 * K * (q + 1)])
+            if q == 1:
+                nc.sync.dma_start(out=b_sb[:, TG:], in_=b[TG:].partition_broadcast(P))
 
+        sel = keep.tile([P, P], F32, name="sel")
+        nc.gpsimd.memset(sel[:], 1.0)
+        nc.gpsimd.affine_select(
+            out=sel[:], in_=sel[:], pattern=[[1, P]], compare_op=ALU.is_ge, fill=0.0, base=0, channel_multiplier=-8
+        )
+        nc.gpsimd.affine_select(
+            out=sel[:], in_=sel[:], pattern=[[-1, P]], compare_op=ALU.is_ge, fill=0.0, base=7, channel_multiplier=8
+        )
+        first_row = keep.tile([P, P], BF16, name="first_row")
+        nc.gpsimd.memset(first_row[:], 0.0)
+        nc.gpsimd.memset(first_row[0:1, :], 1.0)
         ident = keep.tile([P, P], F32, name="ident")
         make_identity(nc, ident[:])
-        mask = keep.tile([P, NR], F32, name="mask")
-        nc.gpsimd.memset(mask[:], 1.0)
-        nc.gpsimd.affine_select(
-            out=mask[:], in_=mask[:], pattern=[[-8, NR]], compare_op=ALU.is_ge, fill=0.0, base=0, channel_multiplier=1
-        )
-        nc.gpsimd.affine_select(
-            out=mask[:], in_=mask[:], pattern=[[8, NR]], compare_op=ALU.is_ge, fill=0.0, base=7, channel_multiplier=-1
-        )
-        qs_m = keep.tile([P, NJ, NR], F32, name="qs_m")
-        nc.vector.tensor_tensor(
-            out=qs_m[:],
-            in0=qs_all[:].rearrange("p (i j) -> p j i", j=NJ),
-            in1=mask[:].unsqueeze(1).to_broadcast([P, NJ, NR]),
-            op=ALU.mult,
-        )
+        qs_bank = acc_pool.tile([P, TG], F32, name="qs_bank", tag="bank")
+        nc.tensor.matmul(qs_bank[:, 0:NJ], lhsT=sel[:], rhs=qs_in[:], start=True, stop=True)
         qs = keep.tile([P, NJ], F32, name="qs")
-        nc.vector.tensor_reduce(out=qs[:], in_=qs_m[:], axis=AX.X, op=ALU.add)
+        nc.vector.tensor_copy(out=qs[:], in_=qs_bank[:, 0:NJ])
         tau_f = keep.tile([P, NR], F32, name="tau_f")
         nc.vector.tensor_copy(out=tau_f[:], in_=tau_b[:])
 
@@ -93,9 +94,6 @@ def tile_absorbed_mla_cache_logits_d2_kernel(
             q_scales.append(keep.tile([P, 4 * P], U8, name="qsc%d" % q, align_bytes=64))
         mx = keep.tile([P, NR], F32, name="mx")
         mx2 = keep.tile([P, NR, 2], F32, name="mx2")
-        first_row = keep.tile([P, P], BF16, name="first_row")
-        nc.gpsimd.memset(first_row[:], 0.0)
-        nc.gpsimd.memset(first_row[0:1, :], 1.0)
 
         def widen(dst, src, col, on_vector):
             if on_vector:
@@ -146,23 +144,14 @@ def tile_absorbed_mla_cache_logits_d2_kernel(
         def widen_q(q, c, js, on_vector):
             if q not in wide_q:
                 wide_q[q] = wide.tile([P, 4 * K], BF16, name="w", align_bytes=64)
-            src, off = (qb0, 0) if q == 0 else (qb1, 4 * B * (q - 1))
             for j in js:
-                if on_vector:
-                    nc.vector.tensor_scalar(
-                        out=wide_q[q][:].rearrange("p (c k) -> p c k", c=4)[:, :, B * j : B * (j + 1)],
-                        in0=src[:, j, off : off + 4 * B].bitcast(FP8).rearrange("p (c k) -> p c k", c=4),
-                        scalar1=qs[:, j : j + 1],
-                        scalar2=None,
-                        op0=ALU.mult,
-                    )
-                else:
-                    nc.scalar.activation(
-                        out=wide_q[q][:, K * c + B * j : K * c + B * (j + 1)],
-                        in_=src[:, j, off + B * c : off + B * (c + 1)].bitcast(FP8),
-                        func=ACT.Copy,
-                        scale=qs[:, j : j + 1],
-                    )
+                i = NJ * c + j
+                widen(
+                    wide_q[q][:, B * i : B * (i + 1)],
+                    qb[q][:, B * i : B * (i + 1)].bitcast(FP8),
+                    qs[:, j : j + 1],
+                    on_vector,
+                )
 
         def turn_q(q, h, on_vector):
             if q not in gath_q:
@@ -224,7 +213,7 @@ def tile_absorbed_mla_cache_logits_d2_kernel(
             nc.scalar.activation(out=x[:], in_=accs[c, g][:], func=ACT.Copy, scale=tau_f[:, c : c + 1])
             acc = acc_pool.tile([P, TG], F32, name="acc_p", bufs=NPB)
             nc.tensor.matmul(acc[:], lhsT=ident[:], rhs=x[:], start=True, stop=False)
-            nc.tensor.matmul(acc[:], lhsT=first_row[:], rhs=b_sb[:, cols], start=False, stop=True)
+            nc.tensor.matmul(acc[:], lhsT=first_row[:], rhs=b_row[:], start=False, stop=True)
             accs[c, g] = acc
 
         def leave_p(c, g):
@@ -254,15 +243,22 @@ def tile_absorbed_mla_cache_logits_d2_kernel(
         LEAD = 3
         LAG = 2
 
+        def spread_b(on_vector):
+            bank = acc_pool.tile([P, TG], F32, name="b_bank", tag="bank")
+            nc.tensor.matmul(bank[:], lhsT=first_row[:], rhs=b_row[:], start=True, stop=True)
+            copy_out(b_sb[:, 0:TG], bank[:], on_vector)
+
         widen_c(0, (0, 1, 2, 3, 8, 9, 10, 11), False)
         widen_c(0, (4, 5, 6, 7, 12, 13, 14, 15), True)
-        widen_q(0, 0, range(4), True)
+        for c in range(4):
+            widen_q(0, c, range(4), True)
         widen_c(1, ON_S, False)
         widen_c(1, ON_V, True)
         turn_c(0, 0, False)
         turn_c(0, 1, True)
         turn_q(0, 0, False)
         turn_q(0, 1, False)
+        spread_b(True)
         widen_c(2, ON_S, False)
         widen_c(2, ON_V, True)
         quantize_c(0)

from contextlib import ExitStack

import concourse.mybir as mybir
from concourse.masks import make_identity

N, T, K, B = 2048, 2048, 512, 128
FLOPS = 2 * N * T * K

F32 = mybir.dt.float32
BF16 = mybir.dt.bfloat16
U32 = mybir.dt.uint32
U8 = mybir.dt.uint8
FP8 = mybir.dt.float8_e4m3fn
FP8X4 = mybir.dt.float8_e4m3fn_x4
ALU = mybir.AluOpType
ACT = mybir.ActivationFunctionType
AX = mybir.AxisListType

P = 128
TG = 512
NG = T // TG
NR = N // P
NJ = K // B
NPB = 1


def tile_absorbed_mla_cache_logits_d2_kernel(
    tc, C_bytes, C_scale, Q_bytes, Q_scale, tau, b, out_0, out_1
):
    nc = tc.nc
    with ExitStack() as ctx:
        keep = ctx.enter_context(tc.tile_pool(name="keep", bufs=1))
        wide = ctx.enter_context(tc.tile_pool(name="wide", bufs=3))
        grp = ctx.enter_context(tc.tile_pool(name="grp", bufs=3))
        outs = ctx.enter_context(tc.tile_pool(name="outs", bufs=1))
        acc_pool = ctx.enter_context(tc.psum_pool(name="accs", bufs=7))
        xs_pool = ctx.enter_context(tc.tile_pool(name="xs", bufs=2))

        cs = keep.tile([P, NG, 4 * NJ], F32, name="cs")
        cs_view = C_scale.rearrange("(g p c) j -> p g (c j)", p=P, c=4)
        nc.scalar.dma_start(out=cs[:, 0:1, :], in_=cs_view[:, 0:1, :])
        qs_in = keep.tile([P, NJ], F32, name="qs_in")
        nc.vector.memset(qs_in[:], 0.0)
        nc.scalar.dma_start(out=qs_in[0:NR, :], in_=Q_scale)
        nc.scalar.dma_start(out=cs[:, 1:NG, :], in_=cs_view[:, 1:NG, :])
        tau_b = keep.tile([P, NR], BF16, name="tau_b")
        nc.scalar.dma_start(out=tau_b[:], in_=tau.rearrange("(p c) -> p c", c=NR))

        c_view = C_bytes.rearrange("(g p c) k -> g p (c k)", p=P, c=4)
        q_view = Q_bytes.rearrange("(p c) k -> p (c k)", c=NR)
        cb, qb = [], []
        for g in range(NG):
            cb.append(keep.tile([P, 4 * K], U8, name="cb%d" % g, align_bytes=64))
            qb.append(keep.tile([P, 4 * K], U8, name="qb%d" % g, align_bytes=64))
        b_sb = keep.tile([P, T], BF16, name="b_sb")
        b_row = keep.tile([P, TG], BF16, name="b_row")
        nc.vector.memset(b_row[:], 0.0)
        nc.scalar.dma_start(out=b_row[0:1, :], in_=b[0:TG].unsqueeze(0))
        nc.sync.dma_start(out=cb[0][:], in_=c_view[0])
        nc.sync.dma_start(out=qb[0][:], in_=q_view[:, 0 : 4 * K])
        for g in range(1, NG):
            nc.sync.dma_start(out=cb[g][:], in_=c_view[g])
        for q in range(1, NG):
            nc.sync.dma_start(out=qb[q][:], in_=q_view[:, 4 * K * q : 4 * K * (q + 1)])
            if q == 1:
                nc.sync.dma_start(out=b_sb[:, TG:], in_=b[TG:].partition_broadcast(P))

        sel = keep.tile([P, P], F32, name="sel")
        nc.gpsimd.memset(sel[:], 1.0)
        nc.gpsimd.affine_select(
            out=sel[:], in_=sel[:], pattern=[[1, P]], compare_op=ALU.is_ge, fill=0.0, base=0, channel_multiplier=-8
        )
        nc.gpsimd.affine_select(
            out=sel[:], in_=sel[:], pattern=[[-1, P]], compare_op=ALU.is_ge, fill=0.0, base=7, channel_multiplier=8
        )
        first_row = keep.tile([P, P], BF16, name="first_row")
        nc.gpsimd.memset(first_row[:], 0.0)
        nc.gpsimd.memset(first_row[0:1, :], 1.0)
        ident = keep.tile([P, P], F32, name="ident")
        make_identity(nc, ident[:])
        qs_bank = acc_pool.tile([P, TG], F32, name="qs_bank", tag="bank")
        nc.tensor.matmul(qs_bank[:, 0:NJ], lhsT=sel[:], rhs=qs_in[:], start=True, stop=True)
        qs = keep.tile([P, NJ], F32, name="qs")
        nc.vector.tensor_copy(out=qs[:], in_=qs_bank[:, 0:NJ])
        tau_f = keep.tile([P, NR], F32, name="tau_f")
        nc.vector.tensor_copy(out=tau_f[:], in_=tau_b[:])

        c_codes, c_scales, q_codes, q_scales = [], [], [], []
        for g in range(NG):
            c_codes.append(keep.tile([P, TG], U32, name="cc%d" % g, align_bytes=64))
            c_scales.append(keep.tile([P, TG], U8, name="csc%d" % g, align_bytes=64))
        for q in range(NR // 4):
            q_codes.append(keep.tile([P, 4 * P], U32, name="qc%d" % q, align_bytes=64))
            q_scales.append(keep.tile([P, 4 * P], U8, name="qsc%d" % q, align_bytes=64))
        mx = keep.tile([P, NR], F32, name="mx")
        mx2 = keep.tile([P, NR, 2], F32, name="mx2")

        def widen(dst, src, col, on_vector):
            if on_vector:
                nc.vector.tensor_scalar(out=dst, in0=src, scalar1=col, scalar2=None, op0=ALU.mult)
            else:
                nc.scalar.activation(out=dst, in_=src, func=ACT.Copy, scale=col)

        def turn(words, pair, first):
            bank = acc_pool.tile([P, 4, P], F32, name="bank", tag="bank")
            for c in range(2):
                for u in range(2):
                    w0 = 256 * (first + c)
                    nc.tensor.transpose(bank[:, 2 * c + u, :], words[:, w0 + u : w0 + 256 : 2], ident[:])
            return bank

        def copy_out(dst, src, on_vector):
            if on_vector:
                nc.vector.tensor_copy(out=dst, in_=src)
            else:
                nc.scalar.copy(out=dst, in_=src)

        wide_c, gath_c, wide_q, gath_q = {}, {}, {}, {}

        def widen_c(g, pieces, on_vector):
            if g not in wide_c:
                wide_c[g] = wide.tile([P, 4 * K], BF16, name="w", align_bytes=64)
                gath_c[g] = grp.tile([P, TG, 4], BF16, name="gt", align_bytes=64)
            for i in pieces:
                widen(
                    wide_c[g][:, B * i : B * (i + 1)],
                    cb[g][:, B * i : B * (i + 1)].bitcast(FP8),
                    cs[:, g, i : i + 1],
                    on_vector,
                )

        def turn_c(g, h, on_vector):
            gw = gath_c[g][:].rearrange("p n t -> p (n t)").bitcast(F32).rearrange("p (r q) -> p r q", q=8)
            bank = turn(wide_c[g][:].bitcast(F32), h, 2 * h)
            copy_out(gw[:, :, 4 * h : 4 * h + 4], bank[:].rearrange("p q r -> p r q"), on_vector)

        def quantize_c(g):
            nc.vector.quantize_mx(
                out=c_codes[g][:].bitcast(FP8X4),
                scales=c_scales[g][:],
                in_=gath_c[g][:].rearrange("p n t -> p (n t)"),
            )

        def widen_q(q, c, js, on_vector):
            if q not in wide_q:
                wide_q[q] = wide.tile([P, 4 * K], BF16, name="w", align_bytes=64)
            for j in js:
                i = NJ * c + j
                widen(
                    wide_q[q][:, B * i : B * (i + 1)],
                    qb[q][:, B * i : B * (i + 1)].bitcast(FP8),
                    qs[:, j : j + 1],
                    on_vector,
                )

        def turn_q(q, h, on_vector):
            if q not in gath_q:
                gath_q[q] = grp.tile([P, TG, 4], BF16, name="gt", align_bytes=64)
            gf = gath_q[q][:, 2 * P * h : 2 * P * (h + 1), :].rearrange("p n t -> p (n t)")
            bank = turn(wide_q[q][:].bitcast(F32), 0, 2 * h)
            copy_out(
                gf.bitcast(F32).rearrange("p (c r u) -> p c r u", c=2, u=2),
                bank[:].rearrange("p (c u) r -> p c r u", u=2),
                on_vector,
            )

        def quantize_q(q):
            nc.vector.quantize_mx(
                out=q_codes[q][:].bitcast(FP8X4),
                scales=q_scales[q][:],
                in_=gath_q[q][:].rearrange("p n t -> p (n t)"),
            )

        out_view = out_0.rearrange("(p c) j -> c p j", c=NR)
        tiles, accs = {}, {}

        def mm(c, g):
            acc = acc_pool.tile([P, TG], F32, name="acc", tag="bank")
            cols = slice(P * (c % 4), P * (c % 4 + 1))
            nc.tensor.matmul_mx(
                out=acc[:],
                lhsT=q_codes[c // 4][:, cols].bitcast(FP8X4),
                lhsT_scale=q_scales[c // 4][:, cols],
                rhs=c_codes[g][:].bitcast(FP8X4),
                rhs_scale=c_scales[g][:],
                start=True,
                stop=True,
            )
            accs[c, g] = acc

        def bank_a(c, g):
            cols = slice(TG * g, TG * (g + 1))
            nc.vector.scalar_tensor_tensor(
                out=tiles[c][:, cols],
                in0=accs[c, g][:],
                scalar=tau_f[:, c : c + 1],
                in1=b_sb[:, cols],
                op0=ALU.mult,
                op1=ALU.add,
            )

        def bank_s(c, g):
            cols = slice(TG * g, TG * (g + 1))
            nc.scalar.activation(out=tiles[c][:, cols], in_=accs[c, g][:], func=ACT.Copy, scale=tau_f[:, c : c + 1])

        def add_b(c, g0, n):
            cols = slice(TG * g0, TG * (g0 + n))
            nc.gpsimd.tensor_tensor(out=tiles[c][:, cols], in0=tiles[c][:, cols], in1=b_sb[:, cols], op=ALU.add)

        def bank_p(c, g):
            cols = slice(TG * g, TG * (g + 1))
            x = xs_pool.tile([P, TG], F32, name="x")
            nc.scalar.activation(out=x[:], in_=accs[c, g][:], func=ACT.Copy, scale=tau_f[:, c : c + 1])
            acc = acc_pool.tile([P, TG], F32, name="acc_p", bufs=NPB)
            nc.tensor.matmul(acc[:], lhsT=ident[:], rhs=x[:], start=True, stop=False)
            nc.tensor.matmul(acc[:], lhsT=first_row[:], rhs=b_row[:], start=False, stop=True)
            accs[c, g] = acc

        def leave_p(c, g):
            cols = slice(TG * g, TG * (g + 1))
            nc.vector.tensor_scalar(
                out=tiles[c][:, cols],
                in0=accs[c, g][:],
                scalar1=1.0,
                scalar2=None,
                op0=ALU.mult,
                op1=ALU.max,
                accum_out=mx2[:, c, 1:2],
            )

        def store(c, g0, n):
            cols = slice(TG * g0, TG * (g0 + n))
            nc.sync.dma_start(out=out_view[c][:, cols], in_=tiles[c][:, cols])

        def row_max(c, g0, n, k):
            cols = slice(TG * g0, TG * (g0 + n))
            nc.vector.tensor_reduce(out=mx2[:, c, k : k + 1], in_=tiles[c][:, cols], axis=AX.X, op=ALU.max)

        for c in range(NR):
            tiles[c] = outs.tile([P, T], F32, name="L%d" % c)
        ON_S, ON_V = (0, 1, 2, 3, 8, 9, 10, 11), (4, 5, 6, 7, 12, 13, 14, 15)
        KIND = ['AAAB', 'AAAB', 'AABB', 'AABB', 'PABB', 'PABB', 'PAAB', 'ABBB', 'PABB', 'PABB', 'PBBB', 'PABB', 'PABB', 'PABB', 'PBBB', 'PABB']
        LEAD = 3
        LAG = 2

        def spread_b(on_vector):
            bank = acc_pool.tile([P, TG], F32, name="b_bank", tag="bank")
            nc.tensor.matmul(bank[:], lhsT=first_row[:], rhs=b_row[:], start=True, stop=True)
            copy_out(b_sb[:, 0:TG], bank[:], on_vector)

        widen_c(0, (0, 1, 2, 3, 8, 9, 10, 11), False)
        widen_c(0, (4, 5, 6, 7, 12, 13, 14, 15), True)
        for c in range(4):
            widen_q(0, c, range(4), True)
        widen_c(1, ON_S, False)
        widen_c(1, ON_V, True)
        turn_c(0, 0, False)
        turn_c(0, 1, True)
        turn_q(0, 0, False)
        turn_q(0, 1, False)
        spread_b(True)
        widen_c(2, ON_S, False)
        widen_c(2, ON_V, True)
        quantize_c(0)
        quantize_q(0)
        turn_c(1, 0, False)
        turn_c(1, 1, False)
        for c in range(4):
            mm(c, 0)
        widen_c(3, ON_S, False)
        widen_c(3, ON_V, True)
        bank_a(0, 0)
        bank_a(1, 0)
        quantize_c(1)
        turn_c(2, 0, False)
        turn_c(2, 1, False)
        bank_a(2, 0)
        bank_a(3, 0)
        for c in range(4):
            store(c, 0, 1)

        def prep(r):
            q, k = r // 4 + 1, r % 4
            if r < 0 or q > 3:
                return
            widen_q(q, k, range(4), False)

        def prep_turn(r):
            q, k = r // 4 + 1, r % 4
            if r >= 0 and q <= 3 and k == 3:
                turn_q(q, 0, False)
                turn_q(q, 1, False)

        def prep_end(r):
            q, k = r // 4 + 1, r % 4
            if r >= 0 and q <= 3 and k == 3:
                quantize_q(q)

        for c in range(2):
            mm(c, 1)
        turn_c(3, 0, False)
        turn_c(3, 1, False)
        quantize_c(2)
        for c in range(2):
            bank_a(c, 1)
            store(c, 1, 1)
        for r in range(LEAD):
            prep(r)
        quantize_c(3)
        done = {(0, 0), (1, 0), (2, 0), (3, 0), (0, 1), (1, 1)}

        def mms(c):
            for g in range(4):
                if (c, g) not in done:
                    mm(c, g)

        mms(0)
        for c in range(NR + LAG):
            if c < NR:
                if KIND[c][0] == "P":
                    bank_p(c, 0)
                nb = KIND[c].count("B")
                for g in range(4 - nb, 4):
                    bank_s(c, g)
                if nb:
                    add_b(c, 4 - nb, nb)
                prep(c + LEAD)
                prep_turn(c + LEAD - 1)
                prep_end(c + LEAD - 2)
                if c + 1 < NR:
                    mms(c + 1)
            if 1 <= c <= NR and KIND[c - 1][0] == "P":
                leave_p(c - 1, 0)
                store(c - 1, 0, KIND[c - 1].count("A") + 1)
            if c < NR:
                for g in range(4):
                    if KIND[c][g] == "A" and (c, g) not in done:
                        bank_a(c, g)
                        if KIND[c][0] == "A":
                            store(c, g, 1)
            if 1 <= c <= NR:
                nb = KIND[c - 1].count("B")
                if nb:
                    store(c - 1, 4 - nb, nb)
            if LAG <= c < NR + LAG:
                if KIND[c - LAG][0] == "P":
                    row_max(c - LAG, 1, 3, 0)
                else:
                    row_max(c - LAG, 0, 2, 0)
                    row_max(c - LAG, 2, 2, 1)
        nc.vector.tensor_reduce(out=mx[:], in_=mx2[:], axis=AX.X, op=ALU.max)
        nc.sync.dma_start(out=out_1.rearrange("(p c) -> p c", c=NR), in_=mx[:])
